import numpy as np
import ml_dtypes


def mxq(x, axis, fmt="e4m3"):
    dtype, down = {"e4m3": (ml_dtypes.float8_e4m3fn, 7), "e5m2": (ml_dtypes.float8_e5m2, 14)}[fmt]
    v = np.moveaxis(np.asarray(x, np.float32).astype(ml_dtypes.bfloat16).astype(np.float64), axis, -1)
    blocks = v.reshape(v.shape[:-1] + (-1, 32))
    amax = np.abs(blocks).max(-1, keepdims=True)
    byte = np.maximum(np.where(amax > 0, np.frexp(amax)[1] - 1 + 127, 0) - down, 1)
    scale = np.exp2(byte - 127.0)
    codes = (blocks / scale).astype(np.float32).astype(dtype).astype(np.float64)
    return np.moveaxis((codes * scale).reshape(v.shape), -1, axis)


WIDE = False


def mx_kscale(k):
    if not WIDE:
        return np.ones(k)
    levels = np.array([10, -10, 5, -5, 0])
    if k % 512:
        return np.exp2(np.random.permutation(np.resize(levels, k // 32))).repeat(32)
    a = np.empty((k // 512, 16))
    for p in range(k // 512):
        a[p, :8] = np.random.permutation(np.resize(levels, 8))
        for g in range(8):
            far = levels[np.abs(levels - a[p, g]) >= 10]
            a[p, g + 8] = far[np.random.randint(len(far))]
    return np.exp2(a.ravel()).repeat(32)


def f64(x):
    return np.asarray(x).astype(np.float64)


def striped(idx):
    return np.tile(np.asarray(idx).reshape(-1, 16).T, (8, 1)).astype(np.uint16)


def unstriped(offs):
    return offs[:16].T.reshape(-1).astype(np.int64)


E2M1 = np.array([0.0, 0.5, 1.0, 1.5, 2.0, 3.0, 4.0, 6.0, -0.0, -0.5, -1.0, -1.5, -2.0, -3.0, -4.0, -6.0])


def pack_weight(w, fmt):
    k, n = w.shape
    w = f64(np.asarray(w, np.float32).astype(ml_dtypes.bfloat16)).reshape(k // 32, 32, n)
    amax = np.abs(w).max(1)
    if fmt == "e4m3":
        byte = np.frexp(amax)[1] - 1 + 127 - 7
    else:
        mant, ex = np.frexp(amax / 6.0)
        byte = np.where(mant > 0.5, ex, ex - 1) + 127
    byte = np.clip(np.where(amax > 0, byte, 1), 1, 254)
    scaled = (w * np.exp2(127.0 - byte)[:, None, :]).reshape(k, n).astype(np.float32)
    by_word = np.ascontiguousarray(scaled.reshape(k // 512, 128, 4, n).transpose(0, 1, 3, 2))
    if fmt == "e4m3":
        words = by_word.astype(ml_dtypes.float8_e4m3fn).view(np.uint8)
    else:
        c = by_word.astype(ml_dtypes.float4_e2m1fn).view(np.uint8) & 0xF
        words = (c[..., 0::2] | (c[..., 1::2] << 4)).reshape(k // 512, 128, 2 * n)
    return np.ascontiguousarray(words), np.ascontiguousarray(byte.astype(np.uint8).reshape(k // 512, 16, n))


def unpack_weight(words, scales, fmt):
    g, _, n = scales.shape
    words = np.ascontiguousarray(words).reshape(g, 128, n, -1)
    if fmt == "e4m3":
        vals = words.view(ml_dtypes.float8_e4m3fn).astype(np.float64)
    else:
        nib = np.empty((g, 128, n, 4), np.uint8)
        nib[..., 0::2] = words & 0xF
        nib[..., 1::2] = words >> 4
        vals = E2M1[nib]
    vals = vals * np.repeat(np.exp2(scales.astype(np.float64) - 127.0), 8, axis=1)[..., None]
    return vals.transpose(0, 1, 3, 2).reshape(g * 512, n)


def sigmoid(v):
    return 1.0 / (1.0 + np.exp(-v))


D, T, I, Q, E, K = 512, 2048, 512, 128, 512, 16


def setup_inputs():
    n = np.random.standard_normal
    idx = np.random.permutation(T)[:I]
    fd = mx_kscale(D)
    fi = mx_kscale(I)
    ti = np.ones(T)
    ti[idx] = fi
    keysp = pack_weight(n((D, T)) / fd[:, None], "e2m1")
    return {
        "query": (n((D, Q)) * 1.0 / np.sqrt(D) * fd[:, None]).astype(np.float32),
        "query2": (n((D, Q)) * 1.0 / np.sqrt(D) * fd[:, None]).astype(np.float32),
        "query3": (n((D, Q)) * 0.8 / np.sqrt(D) * fd[:, None]).astype(np.float32),
        "keys_words": keysp[0],
        "keys_scales": keysp[1],
        "os": (np.random.uniform(4.0, 16.0, (1, I)) * fi).astype(np.float32),
        "vals": (n((E, T)) / ti).astype(np.float32),
        "vsharp": (np.random.uniform(0.6, 1.2, (Q, 1))).astype(np.float32),
        "offs": striped(idx),
    }


def reference(query, query2, query3, keys_words, keys_scales, os, vals, vsharp, offs):
    idx = unstriped(offs)
    keysu = unpack_weight(keys_words, keys_scales, "e2m1")
    queryq = mxq(f64(query), 0, "e4m3")
    keysidxg = keysu[:, idx]
    a = queryq.T @ keysidxg
    query2q = mxq(f64(query2), 0, "e4m3")
    b = query2q.T @ keysidxg
    query3q = mxq(f64(query3), 0, "e4m3")
    b3 = query3q.T @ keysidxg
    s = a * sigmoid(b - b3) + b3
    p = np.exp(s - np.max(s, axis=1, keepdims=True))
    r = p / np.sum(p, axis=1, keepdims=True)
    rt = r.T
    rg = rt.reshape(I, K, Q // K).sum(axis=2)
    rr = np.repeat(rg, Q // K, axis=1)
    w0 = np.square(rt) / rr
    w = w0.T
    wo1 = w * f64(os)
    wt1 = wo1.T
    vt1 = f64(vals)[:, idx].T
    wt1q = mxq(wt1, 0, "e4m3")
    vt1q = mxq(vt1, 0, "e4m3")
    o = wt1q.T @ vt1q
    oz = o * f64(vsharp)
    oe = np.exp(oz - np.max(oz, axis=1, keepdims=True))
    y = oe / np.sum(oe, axis=1, keepdims=True) * 512.0
    return y

@@ -1,0 +1,228 @@
+from contextlib import ExitStack
+
+import concourse.mybir as mybir
+from concourse.masks import make_identity
+
+F32 = mybir.dt.float32
+BF16 = mybir.dt.bfloat16
+I32 = mybir.dt.int32
+U32 = mybir.dt.uint32
+U16 = mybir.dt.uint16
+U8 = mybir.dt.uint8
+FP8X4 = mybir.dt.float8_e4m3fn_x4
+FP4X4 = mybir.dt.float4_e2m1fn_x4
+ACT = mybir.ActivationFunctionType
+ALU = mybir.AluOpType
+AX = mybir.AxisListType
+
+P = 128
+D, T, I, Q, E = 512, 2048, 512, 128, 512
+GROUPS, GROUP = 16, 8
+ET = E // P
+BIG = 1.0e30
+SPLIT = 256
+
+FLOPS = 2 * Q * I * D * 3 + 2 * Q * E * I
+
+
+def tile_attend_threeviews_shared_readshares_kernel(
+    tc, query, query2, query3, keys_words, keys_scales, slot_factor, vals, vsharp, offs, out
+):
+    nc = tc.nc
+    with ExitStack() as ctx:
+        sb = ctx.enter_context(tc.tile_pool(name="sb", bufs=1))
+        lay = ctx.enter_context(tc.tile_pool(name="lay", bufs=1))
+        ps = ctx.enter_context(tc.psum_pool(name="ps", bufs=1))
+
+        offsets = sb.tile([P, I // 16], U16, name="offsets")
+        nc.sync.dma_start(offsets[:], offs)
+        ks_pool = sb.tile([P, T], U8, name="ks_pool", align_bytes=64)
+        nc.vector.memset(ks_pool[:].bitcast(U32), 0)
+        def load_query(n, src):
+            raw = sb.tile([P, 4, Q], F32, name="q_raw%d" % n)
+            nc.sync.dma_start(raw[:], src.rearrange("(p t) q -> p t q", t=4))
+            return raw
+
+        q_raw = [load_query(0, query2)]
+        for c in range(4):
+            (nc.sync, nc.scalar)[c // 2].dma_start(
+                ks_pool[32 * c : 32 * c + 4, :].bitcast(I32),
+                keys_scales[0, 4 * c : 4 * c + 4, :].bitcast(I32),
+            )
+        q_raw.append(load_query(1, query3))
+        kw_pool = sb.tile([P, T], U16, name="kw_pool", align_bytes=64)
+        nc.sync.dma_start(kw_pool[:].bitcast(I32), keys_words[0].bitcast(I32))
+        q_raw.append(load_query(2, query))
+        v_pool = []
+        for j in range(ET):
+            vp = lay.tile([P, T], F32, name="v_pool%d" % j, align_bytes=64, offset=4 * T * j)
+            nc.sync.dma_start(vp[:], vals[j * P : (j + 1) * P, :])
+            v_pool.append(vp)
+        os_t = sb.tile([P, 4], F32, name="os_t")
+        nc.gpsimd.dma_start(os_t[:], slot_factor.rearrange("o (s t) -> (o s) t", t=4))
+        vs = sb.tile([P, 1], F32, name="vs")
+        nc.gpsimd.dma_start(vs[:], vsharp)
+        ident = sb.tile([P, P], F32, name="ident")
+        make_identity(nc, ident[:])
+
+        H = I // 2
+        ks = sb.tile([P, I], U8, name="ks", align_bytes=64)
+        nc.vector.tensor_copy(ks[:], ks_pool[:].indirect(offsets[:]))
+
+        q23 = sb.tile([P, 2, Q, 4], BF16, name="q23", align_bytes=64)
+        q1 = sb.tile([P, Q, 4], BF16, name="q1", align_bytes=64)
+        nc.scalar.activation(q23[:, 0], q_raw[0][:].rearrange("p t q -> p q t"), ACT.Copy)
+        nc.scalar.activation(q23[:, 1], q_raw[1][:].rearrange("p t q -> p q t"), ACT.Copy, scale=-1.0)
+        nc.scalar.activation(q1[:], q_raw[2][:].rearrange("p t q -> p q t"), ACT.Copy)
+        q23c = sb.tile([P, 2 * Q], U32, name="q23c", align_bytes=64)
+        q23s = sb.tile([P, 2 * Q], U8, name="q23s", align_bytes=64)
+        q1c = sb.tile([P, Q], U32, name="q1c", align_bytes=64)
+        q1s = sb.tile([P, Q], U8, name="q1s", align_bytes=64)
+        nc.vector.quantize_mx(out=q23c[:].bitcast(FP8X4), scales=q23s[:], in_=q23[:].rearrange("p n q t -> p (n q t)"))
+        kw = []
+        for h in range(2):
+            kwh = sb.tile([P, H], U16, name="kw%d" % h, align_bytes=64)
+            nc.vector.tensor_copy(kwh[:], kw_pool[:].indirect(offsets[:, h * H // 16 : (h + 1) * H // 16]))
+            kw.append(kwh)
+        nc.vector.quantize_mx(out=q1c[:].bitcast(FP8X4), scales=q1s[:], in_=q1[:].rearrange("p q t -> p (q t)"))
+
+        def score(dst, h, codes, scales, start, stop):
+            nc.tensor.matmul_mx(
+                out=dst, lhsT=codes.bitcast(FP8X4), lhsT_scale=scales,
+                rhs=kw[h][:].bitcast(FP4X4), rhs_scale=ks[:, h * H : (h + 1) * H], start=start, stop=stop,
+            )
+
+        def dealt(cols):
+            return cols.rearrange("q (s t) -> q t s", t=4)
+
+        diff, th, both = [], [], []
+        for h in range(2):
+            d = ps.tile([P, H], F32, name="diff%d" % h, tag="bank%d" % h)
+            score(d[:], h, q23c[:, 0:Q], q23s[:, 0:Q], True, False)
+            score(d[:], h, q23c[:, Q : 2 * Q], q23s[:, Q : 2 * Q], False, True)
+            diff.append(d)
+        for h in range(2):
+            b = ps.tile([P, 2, H], F32, name="both%d" % h, tag="bank%d" % (2 + h))
+            score(b[:, 0, :], h, q23c[:, Q : 2 * Q], q23s[:, Q : 2 * Q], True, True)
+            score(b[:, 1, :], h, q1c[:], q1s[:], True, True)
+            both.append(b)
+        for h in range(2):
+            t_h = sb.tile([P, 4, H // 4], F32, name="th%d" % h, tag="th%d" % h)
+            nc.scalar.activation(t_h[:], dealt(diff[h][:]), ACT.Tanh, scale=0.5)
+            th.append(t_h)
+        ta = sb.tile([P, 2, 4, H // 4], F32, name="ta")
+        for h in range(2):
+            nc.vector.scalar_tensor_tensor(ta[:, h], th[h][:], 1.0, dealt(both[h][:, 1, :]), ALU.add, ALU.mult)
+        ns = sb.tile([P, 2, 4, H // 4], F32, name="ns", tag="vg1", align_bytes=64)
+        for h in range(2):
+            nc.vector.scalar_tensor_tensor(ns[:, h], ta[:, h], -0.5, dealt(both[h][:, 0, :]), ALU.mult, ALU.add)
+        nm = sb.tile([P, 1], F32, name="nm")
+        ns_row = ns[:].rearrange("q h t s -> q (h t s)")
+        nc.vector.tensor_reduce(nm[:], ns_row, AX.X, ALU.min)
+        p = lay.tile([P, 2, 4, H // 4], F32, name="p", align_bytes=64, offset=0)
+        psum_row = sb.tile([P, 1], F32, name="psum_row")
+        nc.scalar.activation(p[:].rearrange("q h t s -> q (h t s)"), ns_row, ACT.Exp, bias=nm[:], scale=-1.0, accum_out=psum_row[:])
+        rinv = sb.tile([P, 1], F32, name="rinv")
+        nc.vector.reciprocal(rinv[:], psum_row[:])
+        p_by_t = p[:].rearrange("q h t s -> q t h s")
+        rt = []
+        for u in range(2):
+            r = sb.tile([P, 2, P], F32, name="r%d" % u, tag="r%d" % u)
+            nc.vector.tensor_scalar(r[:].rearrange("q t (h s) -> q t h s", h=2), p_by_t[:, 2 * u : 2 * u + 2], rinv[:], None, ALU.mult)
+            rt_u = ps.tile([P, 2, Q], F32, name="rt%d" % u, tag="bank%d" % u)
+            for t in range(2):
+                nc.tensor.transpose(rt_u[:, t, :], r[:, t, :], ident[:])
+            rt.append(rt_u)
+        r2 = lay.tile([P, 4, P], F32, name="r2", align_bytes=64, offset=4 * T * 2)
+        nc.scalar.activation(r2[:].rearrange("q t (h s) -> q t h s", h=2), p_by_t, ACT.Square, scale=rinv[:])
+        r2t = ps.tile([P, 4, Q], F32, name="r2t")
+        for t in range(4):
+            nc.tensor.transpose(r2t[:, t, :], r2[:, t, :], ident[:])
+        rg = sb.tile([P, 2, GROUPS, 2], F32, name="rg", tag="vg3", align_bytes=64)
+        for u in range(2):
+            nc.vector.tensor_reduce(rg[:, u], rt[u][:].rearrange("s t (k j) -> s k t j", j=GROUP), AX.X, ALU.add)
+        rginv = sb.tile([P, 2, GROUPS, 2], F32, name="rginv")
+        for u in range(2):
+            nc.vector.reciprocal(rginv[:, u], rg[:, u])
+        vg_last = sb.tile([P, I], BF16, name="vg3", tag="vg3", align_bytes=64)
+        nc.vector.tensor_copy(vg_last[:, 0:SPLIT], v_pool[ET - 1][:].indirect(offsets[:, 0 : SPLIT // 16]))
+        nc.scalar.activation(vg_last[:, SPLIT:I], v_pool[ET - 1][:].indirect(offsets[:, SPLIT // 16 : I // 16]), ACT.Copy)
+
+        f = lay.tile([P, GROUPS, 4], F32, name="f", align_bytes=64, offset=4 * T * 3)
+        for u in range(2):
+            nc.vector.scalar_tensor_tensor(
+                f[:, :, 2 * u : 2 * u + 2], rginv[:, u], BIG,
+                os_t[:, 2 * u : 2 * u + 2].unsqueeze(1).to_broadcast([P, GROUPS, 2]), ALU.min, ALU.mult,
+            )
+
+        wt = sb.tile([P, Q, 4], BF16, name="wt", align_bytes=64)
+        nc.vector.tensor_tensor(
+            wt[:].rearrange("s (k j) t -> s k j t", j=GROUP),
+            r2t[:].rearrange("s t (k j) -> s k j t", j=GROUP),
+            f[:].unsqueeze(2).to_broadcast([P, GROUPS, GROUP, 4]),
+            ALU.mult,
+        )
+        wc = sb.tile([P, Q], U32, name="wc", align_bytes=64)
+        ws = sb.tile([P, Q], U8, name="ws", align_bytes=64)
+        nc.vector.quantize_mx(out=wc[:].bitcast(FP8X4), scales=ws[:], in_=wt[:].rearrange("s q t -> s (q t)"))
+
+        nvs = sb.tile([P, 1], F32, name="nvs")
+        nc.gpsimd.tensor_scalar(nvs[:], vs[:], -1.0, 0.0, ALU.mult, ALU.add)
+
+        def turn(vg, vt):
+            pairs = vg[:].bitcast(F32)
+            for u in range(2):
+                nc.tensor.transpose(vt[:, u, :], pairs[:, u : I // 2 : 2], ident[:])
+
+        def quantise(name, vi, width):
+            codes = sb.tile([P, width], U32, name=name + "_codes", align_bytes=64)
+            scales = sb.tile([P, width], U8, name=name + "_scales", align_bytes=64)
+            nc.vector.quantize_mx(out=codes[:].bitcast(FP8X4), scales=scales[:], in_=vi[:])
+            return codes, scales
+
+        def read(dst, operand):
+            nc.tensor.matmul_mx(
+                out=dst, lhsT=wc[:].bitcast(FP8X4), lhsT_scale=ws[:],
+                rhs=operand[0][:].bitcast(FP8X4), rhs_scale=operand[1][:], start=True, stop=True,
+            )
+
+        HEAD = 3 * P
+        vt_first = ps.tile([P, 2, P], F32, name="vt_first")
+        vt_mid = ps.tile([P, 2, 2, P], F32, name="vt_mid")
+        vt_last = ps.tile([P, 2, P], F32, name="vt_last")
+        for j, vt in enumerate((vt_first[:], vt_mid[:, 0], vt_mid[:, 1])):
+            vg = sb.tile([P, I], BF16, name="vg%d" % j, tag="vg%d" % j, align_bytes=64)
+            nc.scalar.activation(vg[:], v_pool[j][:].indirect(offsets[:]), ACT.Copy)
+            turn(vg, vt)
+        turn(vg_last, vt_last[:])
+        vi_first = sb.tile([P, 4 * P], BF16, name="vi_first", align_bytes=64)
+        nc.scalar.copy(vi_first[:].bitcast(F32).rearrange("s (e u) -> s e u", u=2), vt_first[:].rearrange("s u e -> s e u"))
+        v_first = quantise("v_first", vi_first, P)
+        vi_mid = lay.tile([P, 8 * P], BF16, name="vi_mid", align_bytes=64, offset=4 * T * 3 + 1024)
+        nc.scalar.copy(
+            vi_mid[:].bitcast(F32).rearrange("s (j e u) -> s j e u", j=2, u=2), vt_mid[:].rearrange("s j u e -> s j e u")
+        )
+        v_mid = quantise("v_mid", vi_mid, 2 * P)
+        o_head = ps.tile([P, HEAD], F32, name="o_head", tag="bank2")
+        read(o_head[:, 0:P], v_first)
+        read(o_head[:, P:HEAD], v_mid)
+        noz = sb.tile([P, E], F32, name="noz")
+        nm_head = sb.tile([P, 1], F32, name="nm_head")
+        nm_all = sb.tile([P, 1], F32, name="nm_all")
+
+        nc.vector.tensor_scalar(noz[:, 0:HEAD], o_head[:], nvs[:], None, ALU.mult, ALU.min, accum_out=nm_head[:])
+        vi_last = sb.tile([P, 4 * P], BF16, name="vi_last", align_bytes=64)
+        nc.scalar.copy(vi_last[:].bitcast(F32).rearrange("s (e u) -> s e u", u=2), vt_last[:].rearrange("s u e -> s e u"))
+        v_last = quantise("v_last", vi_last, P)
+        o_last = ps.tile([P, P], F32, name="o_last", tag="bank3")
+        read(o_last[:], v_last)
+        nc.vector.tensor_scalar(noz[:, HEAD:E], o_last[:], nvs[:], nm_head[:], ALU.mult, ALU.min, accum_out=nm_all[:])
+
+        oe = sb.tile([P, E], F32, name="oe")
+        oe_sum = sb.tile([P, 1], F32, name="oe_sum")
+        nc.scalar.activation(oe[:], noz[:], ACT.Exp, bias=nm_all[:], scale=-1.0, accum_out=oe_sum[:])
+        oinv = sb.tile([P, 1], F32, name="oinv")
+        nc.vector.reciprocal(oinv[:], oe_sum[:])
+        y = sb.tile([P, E], F32, name="y")
+        nc.vector.tensor_scalar(y[:], oe[:], oinv[:], float(E), ALU.mult, ALU.mult)
+        nc.sync.dma_start(out, y[:])

@@ -20,7 +20,7 @@ D, T, I, Q, E = 512, 2048, 512, 128, 512
 GROUPS, GROUP = 16, 8
 ET = E // P
 BIG = 1.0e30
-SPLIT = 256
+SPLIT = 288
 
 FLOPS = 2 * Q * I * D * 3 + 2 * Q * E * I
 
@@ -38,21 +38,18 @@ def tile_attend_threeviews_shared_readshares_kernel(
         nc.sync.dma_start(offsets[:], offs)
         ks_pool = sb.tile([P, T], U8, name="ks_pool", align_bytes=64)
         nc.vector.memset(ks_pool[:].bitcast(U32), 0)
-        def load_query(n, src):
-            raw = sb.tile([P, 4, Q], F32, name="q_raw%d" % n)
-            nc.sync.dma_start(raw[:], src.rearrange("(p t) q -> p t q", t=4))
-            return raw
-
-        q_raw = [load_query(0, query2)]
+        kw_pool = sb.tile([P, T], U16, name="kw_pool", align_bytes=64)
+        nc.sync.dma_start(kw_pool[:].bitcast(I32), keys_words[0].bitcast(I32))
         for c in range(4):
             (nc.sync, nc.scalar)[c // 2].dma_start(
                 ks_pool[32 * c : 32 * c + 4, :].bitcast(I32),
                 keys_scales[0, 4 * c : 4 * c + 4, :].bitcast(I32),
             )
-        q_raw.append(load_query(1, query3))
-        kw_pool = sb.tile([P, T], U16, name="kw_pool", align_bytes=64)
-        nc.sync.dma_start(kw_pool[:].bitcast(I32), keys_words[0].bitcast(I32))
-        q_raw.append(load_query(2, query))
+        q_raw = []
+        for n, src in enumerate((query2, query3, query)):
+            raw = sb.tile([P, 4, Q], F32, name="q_raw%d" % n)
+            nc.sync.dma_start(raw[:], src.rearrange("(p t) q -> p t q", t=4))
+            q_raw.append(raw)
         v_pool = []
         for j in range(ET):
             vp = lay.tile([P, T], F32, name="v_pool%d" % j, align_bytes=64, offset=4 * T * j)
@@ -66,56 +63,63 @@ def tile_attend_threeviews_shared_readshares_kernel(
         make_identity(nc, ident[:])
 
         H = I // 2
-        ks = sb.tile([P, I], U8, name="ks", align_bytes=64)
-        nc.vector.tensor_copy(ks[:], ks_pool[:].indirect(offsets[:]))
+        def quantise(name, values, width, codes=None):
+            if codes is None:
+                codes = sb.tile([P, width], U32, name=name + "_codes", align_bytes=64)
+            scales = sb.tile([P, width], U8, name=name + "_scales", align_bytes=64)
+            nc.vector.quantize_mx(out=codes[:].bitcast(FP8X4), scales=scales[:], in_=values[:])
+            return codes, scales
 
-        q23 = sb.tile([P, 2, Q, 4], BF16, name="q23", align_bytes=64)
-        q1 = sb.tile([P, Q, 4], BF16, name="q1", align_bytes=64)
-        nc.scalar.activation(q23[:, 0], q_raw[0][:].rearrange("p t q -> p q t"), ACT.Copy)
-        nc.scalar.activation(q23[:, 1], q_raw[1][:].rearrange("p t q -> p q t"), ACT.Copy, scale=-1.0)
-        nc.scalar.activation(q1[:], q_raw[2][:].rearrange("p t q -> p q t"), ACT.Copy)
-        q23c = sb.tile([P, 2 * Q], U32, name="q23c", align_bytes=64)
-        q23s = sb.tile([P, 2 * Q], U8, name="q23s", align_bytes=64)
-        q1c = sb.tile([P, Q], U32, name="q1c", align_bytes=64)
-        q1s = sb.tile([P, Q], U8, name="q1s", align_bytes=64)
-        nc.vector.quantize_mx(out=q23c[:].bitcast(FP8X4), scales=q23s[:], in_=q23[:].rearrange("p n q t -> p (n q t)"))
-        kw = []
-        for h in range(2):
-            kwh = sb.tile([P, H], U16, name="kw%d" % h, align_bytes=64)
-            nc.vector.tensor_copy(kwh[:], kw_pool[:].indirect(offsets[:, h * H // 16 : (h + 1) * H // 16]))
-            kw.append(kwh)
-        nc.vector.quantize_mx(out=q1c[:].bitcast(FP8X4), scales=q1s[:], in_=q1[:].rearrange("p q t -> p (q t)"))
+        def quantise_query(n, sign):
+            qi = sb.tile([P, 4 * Q], BF16, name="qi%d" % n, tag="qi%d" % n, align_bytes=64)
+            nc.scalar.activation(
+                qi[:].rearrange("p (q t) -> p q t", t=4), q_raw[n][:].rearrange("p t q -> p q t"), ACT.Copy, scale=sign
+            )
+            return quantise("q%d" % n, qi, Q)
 
-        def score(dst, h, codes, scales, start, stop):
+        def gather_keys(name, pool_tile, dtype, h, tag):
+            dst = sb.tile([P, H], dtype, name=name, tag=tag, align_bytes=64)
+            nc.vector.tensor_copy(dst[:], pool_tile[:].indirect(offsets[:, h * H // 16 : (h + 1) * H // 16]))
+            return dst
+
+        kw = [gather_keys("kw%d" % h, kw_pool, U16, h, "kw%d" % h) for h in range(2)]
+        ks = [gather_keys("ks0", ks_pool, U8, 0, "ks0")]
+        q2 = quantise_query(0, 1.0)
+        nq3 = quantise_query(1, -1.0)
+        ks.append(gather_keys("ks1", ks_pool, U8, 1, "qi1"))
+        q1 = quantise_query(2, 1.0)
+
+        def score(dst, h, operand, start, stop):
             nc.tensor.matmul_mx(
-                out=dst, lhsT=codes.bitcast(FP8X4), lhsT_scale=scales,
-                rhs=kw[h][:].bitcast(FP4X4), rhs_scale=ks[:, h * H : (h + 1) * H], start=start, stop=stop,
+                out=dst[:], lhsT=operand[0][:].bitcast(FP8X4), lhsT_scale=operand[1][:],
+                rhs=kw[h][:].bitcast(FP4X4), rhs_scale=ks[h][:], start=start, stop=stop,
             )
 
         def dealt(cols):
             return cols.rearrange("q (s t) -> q t s", t=4)
 
-        diff, th, both = [], [], []
+        diff = [ps.tile([P, H], F32, name="diff%d" % h, tag="bank%d" % h) for h in range(2)]
+        a = [ps.tile([P, H], F32, name="a%d" % h, tag="bank%d" % (2 + h)) for h in range(2)]
+        nb3 = [ps.tile([P, H], F32, name="nb3%d" % h, tag="bank%d" % (4 + h)) for h in range(2)]
         for h in range(2):
-            d = ps.tile([P, H], F32, name="diff%d" % h, tag="bank%d" % h)
-            score(d[:], h, q23c[:, 0:Q], q23s[:, 0:Q], True, False)
-            score(d[:], h, q23c[:, Q : 2 * Q], q23s[:, Q : 2 * Q], False, True)
-            diff.append(d)
+            score(diff[h], h, q2, True, False)
+            score(diff[h], h, nq3, False, True)
+            if h == 0:
+                score(nb3[0], 0, nq3, True, True)
         for h in range(2):
-            b = ps.tile([P, 2, H], F32, name="both%d" % h, tag="bank%d" % (2 + h))
-            score(b[:, 0, :], h, q23c[:, Q : 2 * Q], q23s[:, Q : 2 * Q], True, True)
-            score(b[:, 1, :], h, q1c[:], q1s[:], True, True)
-            both.append(b)
+            score(a[h], h, q1, True, True)
+        score(nb3[1], 1, nq3, True, True)
+        th = []
         for h in range(2):
-            t_h = sb.tile([P, 4, H // 4], F32, name="th%d" % h, tag="th%d" % h)
+            t_h = sb.tile([P, 4, H // 4], F32, name="th%d" % h)
             nc.scalar.activation(t_h[:], dealt(diff[h][:]), ACT.Tanh, scale=0.5)
             th.append(t_h)
         ta = sb.tile([P, 2, 4, H // 4], F32, name="ta")
         for h in range(2):
-            nc.vector.scalar_tensor_tensor(ta[:, h], th[h][:], 1.0, dealt(both[h][:, 1, :]), ALU.add, ALU.mult)
+            nc.vector.scalar_tensor_tensor(ta[:, h], th[h][:], 1.0, dealt(a[h][:]), ALU.add, ALU.mult)
         ns = sb.tile([P, 2, 4, H // 4], F32, name="ns", tag="vg1", align_bytes=64)
         for h in range(2):
-            nc.vector.scalar_tensor_tensor(ns[:, h], ta[:, h], -0.5, dealt(both[h][:, 0, :]), ALU.mult, ALU.add)
+            nc.vector.scalar_tensor_tensor(ns[:, h], ta[:, h], -0.5, dealt(nb3[h][:]), ALU.mult, ALU.add)
         nm = sb.tile([P, 1], F32, name="nm")
         ns_row = ns[:].rearrange("q h t s -> q (h t s)")
         nc.vector.tensor_reduce(nm[:], ns_row, AX.X, ALU.min)
@@ -125,46 +129,46 @@ def tile_attend_threeviews_shared_readshares_kernel(
         rinv = sb.tile([P, 1], F32, name="rinv")
         nc.vector.reciprocal(rinv[:], psum_row[:])
         p_by_t = p[:].rearrange("q h t s -> q t h s")
+        r = sb.tile([P, 4, P], F32, name="r")
         rt = []
         for u in range(2):
-            r = sb.tile([P, 2, P], F32, name="r%d" % u, tag="r%d" % u)
-            nc.vector.tensor_scalar(r[:].rearrange("q t (h s) -> q t h s", h=2), p_by_t[:, 2 * u : 2 * u + 2], rinv[:], None, ALU.mult)
-            rt_u = ps.tile([P, 2, Q], F32, name="rt%d" % u, tag="bank%d" % u)
+            nc.vector.tensor_scalar(
+                r[:, 2 * u : 2 * u + 2].rearrange("q t (h s) -> q t h s", h=2), p_by_t[:, 2 * u : 2 * u + 2], rinv[:], None, ALU.mult
+            )
+            rt_u = ps.tile([P, 2, Q], F32, name="rt%d" % u, tag="bank%d" % (2 + u))
             for t in range(2):
-                nc.tensor.transpose(rt_u[:, t, :], r[:, t, :], ident[:])
+                nc.tensor.transpose(rt_u[:, t, :], r[:, 2 * u + t, :], ident[:])
             rt.append(rt_u)
-        r2 = lay.tile([P, 4, P], F32, name="r2", align_bytes=64, offset=4 * T * 2)
-        nc.scalar.activation(r2[:].rearrange("q t (h s) -> q t h s", h=2), p_by_t, ACT.Square, scale=rinv[:])
-        r2t = ps.tile([P, 4, Q], F32, name="r2t")
+        r2 = sb.tile([P, 4, P], F32, name="r2")
+        nc.vector.tensor_tensor(r2[:], r[:], r[:], ALU.mult)
+        r2t = ps.tile([P, 4, Q], F32, name="r2t", tag="bank4")
         for t in range(4):
             nc.tensor.transpose(r2t[:, t, :], r2[:, t, :], ident[:])
-        rg = sb.tile([P, 2, GROUPS, 2], F32, name="rg", tag="vg3", align_bytes=64)
+        rg = sb.tile([P, 2, GROUPS, 2], F32, name="rg")
         for u in range(2):
             nc.vector.tensor_reduce(rg[:, u], rt[u][:].rearrange("s t (k j) -> s k t j", j=GROUP), AX.X, ALU.add)
-        rginv = sb.tile([P, 2, GROUPS, 2], F32, name="rginv")
+        rginv = sb.tile([P, 2, GROUPS, 2], F32, name="rginv", tag="vg3", align_bytes=64)
         for u in range(2):
             nc.vector.reciprocal(rginv[:, u], rg[:, u])
-        vg_last = sb.tile([P, I], BF16, name="vg3", tag="vg3", align_bytes=64)
-        nc.vector.tensor_copy(vg_last[:, 0:SPLIT], v_pool[ET - 1][:].indirect(offsets[:, 0 : SPLIT // 16]))
-        nc.scalar.activation(vg_last[:, SPLIT:I], v_pool[ET - 1][:].indirect(offsets[:, SPLIT // 16 : I // 16]), ACT.Copy)
-
-        f = lay.tile([P, GROUPS, 4], F32, name="f", align_bytes=64, offset=4 * T * 3)
+        f = sb.tile([P, GROUPS, 4], F32, name="f")
         for u in range(2):
             nc.vector.scalar_tensor_tensor(
                 f[:, :, 2 * u : 2 * u + 2], rginv[:, u], BIG,
                 os_t[:, 2 * u : 2 * u + 2].unsqueeze(1).to_broadcast([P, GROUPS, 2]), ALU.min, ALU.mult,
             )
 
-        wt = sb.tile([P, Q, 4], BF16, name="wt", align_bytes=64)
+        vg_last = sb.tile([P, I], BF16, name="vg3", tag="vg3", align_bytes=64)
+        nc.vector.tensor_copy(vg_last[:, 0:SPLIT], v_pool[ET - 1][:].indirect(offsets[:, 0 : SPLIT // 16]))
+        nc.scalar.activation(vg_last[:, SPLIT:I], v_pool[ET - 1][:].indirect(offsets[:, SPLIT // 16 : I // 16]), ACT.Copy)
+
+        wt = lay.tile([P, 4 * Q], BF16, name="wt", align_bytes=64, offset=4 * T * 3)
         nc.vector.tensor_tensor(
-            wt[:].rearrange("s (k j) t -> s k j t", j=GROUP),
+            wt[:].rearrange("s (k j t) -> s k j t", j=GROUP, t=4),
             r2t[:].rearrange("s t (k j) -> s k j t", j=GROUP),
             f[:].unsqueeze(2).to_broadcast([P, GROUPS, GROUP, 4]),
             ALU.mult,
         )
-        wc = sb.tile([P, Q], U32, name="wc", align_bytes=64)
-        ws = sb.tile([P, Q], U8, name="ws", align_bytes=64)
-        nc.vector.quantize_mx(out=wc[:].bitcast(FP8X4), scales=ws[:], in_=wt[:].rearrange("s q t -> s (q t)"))
+        wc, ws = quantise("w", wt, Q)
 
         nvs = sb.tile([P, 1], F32, name="nvs")
         nc.gpsimd.tensor_scalar(nvs[:], vs[:], -1.0, 0.0, ALU.mult, ALU.add)
@@ -174,12 +178,6 @@ def tile_attend_threeviews_shared_readshares_kernel(
             for u in range(2):
                 nc.tensor.transpose(vt[:, u, :], pairs[:, u : I // 2 : 2], ident[:])
 
-        def quantise(name, vi, width):
-            codes = sb.tile([P, width], U32, name=name + "_codes", align_bytes=64)
-            scales = sb.tile([P, width], U8, name=name + "_scales", align_bytes=64)
-            nc.vector.quantize_mx(out=codes[:].bitcast(FP8X4), scales=scales[:], in_=vi[:])
-            return codes, scales
-
         def read(dst, operand):
             nc.tensor.matmul_mx(
                 out=dst, lhsT=wc[:].bitcast(FP8X4), lhsT_scale=ws[:],
@@ -187,34 +185,34 @@ def tile_attend_threeviews_shared_readshares_kernel(
             )
 
         HEAD = 3 * P
-        vt_first = ps.tile([P, 2, P], F32, name="vt_first")
-        vt_mid = ps.tile([P, 2, 2, P], F32, name="vt_mid")
+        def interleave(vi, vt, copy):
+            copy(vi[:].bitcast(F32).rearrange("s (e u) -> s e u", u=2), vt[:].rearrange("s u e -> s e u"))
+
+        o_head = ps.tile([P, HEAD], F32, name="o_head", tag="bank5")
         vt_last = ps.tile([P, 2, P], F32, name="vt_last")
-        for j, vt in enumerate((vt_first[:], vt_mid[:, 0], vt_mid[:, 1])):
+        turn(vg_last, vt_last[:])
+        for j in range(ET - 1):
             vg = sb.tile([P, I], BF16, name="vg%d" % j, tag="vg%d" % j, align_bytes=64)
             nc.scalar.activation(vg[:], v_pool[j][:].indirect(offsets[:]), ACT.Copy)
-            turn(vg, vt)
-        turn(vg_last, vt_last[:])
-        vi_first = sb.tile([P, 4 * P], BF16, name="vi_first", align_bytes=64)
-        nc.scalar.copy(vi_first[:].bitcast(F32).rearrange("s (e u) -> s e u", u=2), vt_first[:].rearrange("s u e -> s e u"))
-        v_first = quantise("v_first", vi_first, P)
-        vi_mid = lay.tile([P, 8 * P], BF16, name="vi_mid", align_bytes=64, offset=4 * T * 3 + 1024)
-        nc.scalar.copy(
-            vi_mid[:].bitcast(F32).rearrange("s (j e u) -> s j e u", j=2, u=2), vt_mid[:].rearrange("s j u e -> s j e u")
-        )
-        v_mid = quantise("v_mid", vi_mid, 2 * P)
-        o_head = ps.tile([P, HEAD], F32, name="o_head", tag="bank2")
-        read(o_head[:, 0:P], v_first)
-        read(o_head[:, P:HEAD], v_mid)
+            vt = ps.tile([P, 2, P], F32, name="vt%d" % j, tag="bank%d" % (0, 2, 3)[j])
+            turn(vg, vt[:])
+            if j == 0:
+                vi = sb.tile([P, 4 * P], BF16, name="vi0", align_bytes=64)
+                interleave(vi, vt, nc.vector.tensor_copy)
+            else:
+                vi = lay.tile([P, 4 * P], BF16, name="vi%d" % j, align_bytes=64, offset=4 * T * (j + 1) + 1024)
+                interleave(vi, vt, nc.scalar.copy)
+            codes = lay.tile([P, P], U32, name="v1_codes", align_bytes=64, offset=4 * T * 3 + 2048) if j == 1 else None
+            read(o_head[:, j * P : (j + 1) * P], quantise("v%d" % j, vi, P, codes))
         noz = sb.tile([P, E], F32, name="noz")
         nm_head = sb.tile([P, 1], F32, name="nm_head")
         nm_all = sb.tile([P, 1], F32, name="nm_all")
 
         nc.vector.tensor_scalar(noz[:, 0:HEAD], o_head[:], nvs[:], None, ALU.mult, ALU.min, accum_out=nm_head[:])
         vi_last = sb.tile([P, 4 * P], BF16, name="vi_last", align_bytes=64)
-        nc.scalar.copy(vi_last[:].bitcast(F32).rearrange("s (e u) -> s e u", u=2), vt_last[:].rearrange("s u e -> s e u"))
+        interleave(vi_last, vt_last, nc.scalar.copy)
         v_last = quantise("v_last", vi_last, P)
-        o_last = ps.tile([P, P], F32, name="o_last", tag="bank3")
+        o_last = ps.tile([P, P], F32, name="o_last")
         read(o_last[:], v_last)
         nc.vector.tensor_scalar(noz[:, HEAD:E], o_last[:], nvs[:], nm_head[:], ALU.mult, ALU.min, accum_out=nm_all[:])
 
@@ -224,5 +222,7 @@ def tile_attend_threeviews_shared_readshares_kernel(
         oinv = sb.tile([P, 1], F32, name="oinv")
         nc.vector.reciprocal(oinv[:], oe_sum[:])
         y = sb.tile([P, E], F32, name="y")
-        nc.vector.tensor_scalar(y[:], oe[:], oinv[:], float(E), ALU.mult, ALU.mult)
-        nc.sync.dma_start(out, y[:])
+        for h, queue in enumerate((nc.sync, nc.scalar)):
+            cols = slice(h * E // 2, (h + 1) * E // 2)
+            nc.vector.tensor_scalar(y[:, cols], oe[:, cols], oinv[:], float(E), ALU.mult, ALU.mult)
+            queue.dma_start(out[:, cols], y[:, cols])

from contextlib import ExitStack

import concourse.mybir as mybir
from concourse.masks import make_identity

F32 = mybir.dt.float32
BF16 = mybir.dt.bfloat16
I32 = mybir.dt.int32
U32 = mybir.dt.uint32
U16 = mybir.dt.uint16
U8 = mybir.dt.uint8
FP8X4 = mybir.dt.float8_e4m3fn_x4
FP4X4 = mybir.dt.float4_e2m1fn_x4
ACT = mybir.ActivationFunctionType
ALU = mybir.AluOpType
AX = mybir.AxisListType

P = 128
D, T, I, Q, E = 512, 2048, 512, 128, 512
GROUPS, GROUP = 16, 8
ET = E // P
BIG = 1.0e30
SPLIT = 288

FLOPS = 2 * Q * I * D * 3 + 2 * Q * E * I


def tile_attend_threeviews_shared_readshares_kernel(
    tc, query, query2, query3, keys_words, keys_scales, slot_factor, vals, vsharp, offs, out
):
    nc = tc.nc
    with ExitStack() as ctx:
        sb = ctx.enter_context(tc.tile_pool(name="sb", bufs=1))
        lay = ctx.enter_context(tc.tile_pool(name="lay", bufs=1))
        ps = ctx.enter_context(tc.psum_pool(name="ps", bufs=1))

        offsets = sb.tile([P, I // 16], U16, name="offsets")
        nc.sync.dma_start(offsets[:], offs)
        ks_pool = sb.tile([P, T], U8, name="ks_pool", align_bytes=64)
        nc.vector.memset(ks_pool[:].bitcast(U32), 0)
        kw_pool = sb.tile([P, T], U16, name="kw_pool", align_bytes=64)
        nc.sync.dma_start(kw_pool[:].bitcast(I32), keys_words[0].bitcast(I32))
        for c in range(4):
            (nc.sync, nc.scalar)[c // 2].dma_start(
                ks_pool[32 * c : 32 * c + 4, :].bitcast(I32),
                keys_scales[0, 4 * c : 4 * c + 4, :].bitcast(I32),
            )
        q_raw = []
        for n, src in enumerate((query2, query3, query)):
            raw = sb.tile([P, 4, Q], F32, name="q_raw%d" % n)
            nc.sync.dma_start(raw[:], src.rearrange("(p t) q -> p t q", t=4))
            q_raw.append(raw)
        v_pool = []
        for j in range(ET):
            vp = lay.tile([P, T], F32, name="v_pool%d" % j, align_bytes=64, offset=4 * T * j)
            nc.sync.dma_start(vp[:], vals[j * P : (j + 1) * P, :])
            v_pool.append(vp)
        os_t = sb.tile([P, 4], F32, name="os_t")
        nc.gpsimd.dma_start(os_t[:], slot_factor.rearrange("o (s t) -> (o s) t", t=4))
        vs = sb.tile([P, 1], F32, name="vs")
        nc.gpsimd.dma_start(vs[:], vsharp)
        ident = sb.tile([P, P], F32, name="ident")
        make_identity(nc, ident[:])

        H = I // 2
        def quantise(name, values, width, codes=None):
            if codes is None:
                codes = sb.tile([P, width], U32, name=name + "_codes", align_bytes=64)
            scales = sb.tile([P, width], U8, name=name + "_scales", align_bytes=64)
            nc.vector.quantize_mx(out=codes[:].bitcast(FP8X4), scales=scales[:], in_=values[:])
            return codes, scales

        def quantise_query(n, sign):
            qi = sb.tile([P, 4 * Q], BF16, name="qi%d" % n, tag="qi%d" % n, align_bytes=64)
            nc.scalar.activation(
                qi[:].rearrange("p (q t) -> p q t", t=4), q_raw[n][:].rearrange("p t q -> p q t"), ACT.Copy, scale=sign
            )
            return quantise("q%d" % n, qi, Q)

        def gather_keys(name, pool_tile, dtype, h, tag):
            dst = sb.tile([P, H], dtype, name=name, tag=tag, align_bytes=64)
            nc.vector.tensor_copy(dst[:], pool_tile[:].indirect(offsets[:, h * H // 16 : (h + 1) * H // 16]))
            return dst

        kw = [gather_keys("kw%d" % h, kw_pool, U16, h, "kw%d" % h) for h in range(2)]
        ks = [gather_keys("ks0", ks_pool, U8, 0, "ks0")]
        q2 = quantise_query(0, 1.0)
        nq3 = quantise_query(1, -1.0)
        ks.append(gather_keys("ks1", ks_pool, U8, 1, "qi1"))
        q1 = quantise_query(2, 1.0)

        def score(dst, h, operand, start, stop):
            nc.tensor.matmul_mx(
                out=dst[:], lhsT=operand[0][:].bitcast(FP8X4), lhsT_scale=operand[1][:],
                rhs=kw[h][:].bitcast(FP4X4), rhs_scale=ks[h][:], start=start, stop=stop,
            )

        def dealt(cols):
            return cols.rearrange("q (s t) -> q t s", t=4)

        diff = [ps.tile([P, H], F32, name="diff%d" % h, tag="bank%d" % h) for h in range(2)]
        a = [ps.tile([P, H], F32, name="a%d" % h, tag="bank%d" % (2 + h)) for h in range(2)]
        nb3 = [ps.tile([P, H], F32, name="nb3%d" % h, tag="bank%d" % (4 + h)) for h in range(2)]
        for h in range(2):
            score(diff[h], h, q2, True, False)
            score(diff[h], h, nq3, False, True)
            if h == 0:
                score(nb3[0], 0, nq3, True, True)
        for h in range(2):
            score(a[h], h, q1, True, True)
        score(nb3[1], 1, nq3, True, True)
        th = []
        for h in range(2):
            t_h = sb.tile([P, 4, H // 4], F32, name="th%d" % h)
            nc.scalar.activation(t_h[:], dealt(diff[h][:]), ACT.Tanh, scale=0.5)
            th.append(t_h)
        ta = sb.tile([P, 2, 4, H // 4], F32, name="ta")
        for h in range(2):
            nc.vector.scalar_tensor_tensor(ta[:, h], th[h][:], 1.0, dealt(a[h][:]), ALU.add, ALU.mult)
        ns = sb.tile([P, 2, 4, H // 4], F32, name="ns", tag="vg1", align_bytes=64)
        for h in range(2):
            nc.vector.scalar_tensor_tensor(ns[:, h], ta[:, h], -0.5, dealt(nb3[h][:]), ALU.mult, ALU.add)
        nm = sb.tile([P, 1], F32, name="nm")
        ns_row = ns[:].rearrange("q h t s -> q (h t s)")
        nc.vector.tensor_reduce(nm[:], ns_row, AX.X, ALU.min)
        p = lay.tile([P, 2, 4, H // 4], F32, name="p", align_bytes=64, offset=0)
        psum_row = sb.tile([P, 1], F32, name="psum_row")
        nc.scalar.activation(p[:].rearrange("q h t s -> q (h t s)"), ns_row, ACT.Exp, bias=nm[:], scale=-1.0, accum_out=psum_row[:])
        rinv = sb.tile([P, 1], F32, name="rinv")
        nc.vector.reciprocal(rinv[:], psum_row[:])
        p_by_t = p[:].rearrange("q h t s -> q t h s")
        r = sb.tile([P, 4, P], F32, name="r")
        rt = []
        for u in range(2):
            nc.vector.tensor_scalar(
                r[:, 2 * u : 2 * u + 2].rearrange("q t (h s) -> q t h s", h=2), p_by_t[:, 2 * u : 2 * u + 2], rinv[:], None, ALU.mult
            )
            rt_u = ps.tile([P, 2, Q], F32, name="rt%d" % u, tag="bank%d" % (2 + u))
            for t in range(2):
                nc.tensor.transpose(rt_u[:, t, :], r[:, 2 * u + t, :], ident[:])
            rt.append(rt_u)
        r2 = sb.tile([P, 4, P], F32, name="r2")
        nc.vector.tensor_tensor(r2[:], r[:], r[:], ALU.mult)
        r2t = ps.tile([P, 4, Q], F32, name="r2t", tag="bank4")
        for t in range(4):
            nc.tensor.transpose(r2t[:, t, :], r2[:, t, :], ident[:])
        rg = sb.tile([P, 2, GROUPS, 2], F32, name="rg")
        for u in range(2):
            nc.vector.tensor_reduce(rg[:, u], rt[u][:].rearrange("s t (k j) -> s k t j", j=GROUP), AX.X, ALU.add)
        rginv = sb.tile([P, 2, GROUPS, 2], F32, name="rginv", tag="vg3", align_bytes=64)
        for u in range(2):
            nc.vector.reciprocal(rginv[:, u], rg[:, u])
        f = sb.tile([P, GROUPS, 4], F32, name="f")
        for u in range(2):
            nc.vector.scalar_tensor_tensor(
                f[:, :, 2 * u : 2 * u + 2], rginv[:, u], BIG,
                os_t[:, 2 * u : 2 * u + 2].unsqueeze(1).to_broadcast([P, GROUPS, 2]), ALU.min, ALU.mult,
            )

        vg_last = sb.tile([P, I], BF16, name="vg3", tag="vg3", align_bytes=64)
        nc.vector.tensor_copy(vg_last[:, 0:SPLIT], v_pool[ET - 1][:].indirect(offsets[:, 0 : SPLIT // 16]))
        nc.scalar.activation(vg_last[:, SPLIT:I], v_pool[ET - 1][:].indirect(offsets[:, SPLIT // 16 : I // 16]), ACT.Copy)

        wt = lay.tile([P, 4 * Q], BF16, name="wt", align_bytes=64, offset=4 * T * 3)
        nc.vector.tensor_tensor(
            wt[:].rearrange("s (k j t) -> s k j t", j=GROUP, t=4),
            r2t[:].rearrange("s t (k j) -> s k j t", j=GROUP),
            f[:].unsqueeze(2).to_broadcast([P, GROUPS, GROUP, 4]),
            ALU.mult,
        )
        wc, ws = quantise("w", wt, Q)

        nvs = sb.tile([P, 1], F32, name="nvs")
        nc.gpsimd.tensor_scalar(nvs[:], vs[:], -1.0, 0.0, ALU.mult, ALU.add)

        def turn(vg, vt):
            pairs = vg[:].bitcast(F32)
            for u in range(2):
                nc.tensor.transpose(vt[:, u, :], pairs[:, u : I // 2 : 2], ident[:])

        def read(dst, operand):
            nc.tensor.matmul_mx(
                out=dst, lhsT=wc[:].bitcast(FP8X4), lhsT_scale=ws[:],
                rhs=operand[0][:].bitcast(FP8X4), rhs_scale=operand[1][:], start=True, stop=True,
            )

        HEAD = 3 * P
        def interleave(vi, vt, copy):
            copy(vi[:].bitcast(F32).rearrange("s (e u) -> s e u", u=2), vt[:].rearrange("s u e -> s e u"))

        o_head = ps.tile([P, HEAD], F32, name="o_head", tag="bank5")
        vt_last = ps.tile([P, 2, P], F32, name="vt_last")
        turn(vg_last, vt_last[:])
        for j in range(ET - 1):
            vg = sb.tile([P, I], BF16, name="vg%d" % j, tag="vg%d" % j, align_bytes=64)
            nc.scalar.activation(vg[:], v_pool[j][:].indirect(offsets[:]), ACT.Copy)
            vt = ps.tile([P, 2, P], F32, name="vt%d" % j, tag="bank%d" % (0, 2, 3)[j])
            turn(vg, vt[:])
            if j == 0:
                vi = sb.tile([P, 4 * P], BF16, name="vi0", align_bytes=64)
                interleave(vi, vt, nc.vector.tensor_copy)
            else:
                vi = lay.tile([P, 4 * P], BF16, name="vi%d" % j, align_bytes=64, offset=4 * T * (j + 1) + 1024)
                interleave(vi, vt, nc.scalar.copy)
            codes = lay.tile([P, P], U32, name="v1_codes", align_bytes=64, offset=4 * T * 3 + 2048) if j == 1 else None
            read(o_head[:, j * P : (j + 1) * P], quantise("v%d" % j, vi, P, codes))
        noz = sb.tile([P, E], F32, name="noz")
        nm_head = sb.tile([P, 1], F32, name="nm_head")
        nm_all = sb.tile([P, 1], F32, name="nm_all")

        nc.vector.tensor_scalar(noz[:, 0:HEAD], o_head[:], nvs[:], None, ALU.mult, ALU.min, accum_out=nm_head[:])
        vi_last = sb.tile([P, 4 * P], BF16, name="vi_last", align_bytes=64)
        interleave(vi_last, vt_last, nc.scalar.copy)
        v_last = quantise("v_last", vi_last, P)
        o_last = ps.tile([P, P], F32, name="o_last")
        read(o_last[:], v_last)
        nc.vector.tensor_scalar(noz[:, HEAD:E], o_last[:], nvs[:], nm_head[:], ALU.mult, ALU.min, accum_out=nm_all[:])

        oe = sb.tile([P, E], F32, name="oe")
        oe_sum = sb.tile([P, 1], F32, name="oe_sum")
        nc.scalar.activation(oe[:], noz[:], ACT.Exp, bias=nm_all[:], scale=-1.0, accum_out=oe_sum[:])
        oinv = sb.tile([P, 1], F32, name="oinv")
        nc.vector.reciprocal(oinv[:], oe_sum[:])
        y = sb.tile([P, E], F32, name="y")
        for h, queue in enumerate((nc.sync, nc.scalar)):
            cols = slice(h * E // 2, (h + 1) * E // 2)
            nc.vector.tensor_scalar(y[:, cols], oe[:, cols], oinv[:], float(E), ALU.mult, ALU.mult)
            queue.dma_start(out[:, cols], y[:, cols])
